import numpy as np
import ml_dtypes

BF16 = ml_dtypes.bfloat16


def bf(x):
    return np.asarray(x, np.float32).astype(BF16)


def f32(x):
    return np.asarray(x, np.float32)


def f64(x):
    return np.asarray(x).astype(np.float64)


def striped(idx):
    return np.concatenate([l.reshape(-1, 16).T for l in idx])


def rows(idx, k):
    return np.tile(np.repeat(idx, 16, axis=0), (k // (16 * 8), 1))


def look(tab, idx):
    return np.take_along_axis(f64(tab), rows(idx, len(tab)), axis=1)


K, S, D, V, N = 256, 2048, 2, 1024, 2048


def setup_inputs():
    return {"tab": f32(np.random.standard_normal((2, K, S))), "t": f32(0.5 * np.random.standard_normal((K, V))), "offs": striped(np.stack([np.random.permutation(S)[:N] for _ in range(8)]))}


def reference(tab, t, offs):
    idx = np.stack([g.T.reshape(-1) for g in np.split(offs, 8)])
    a = [look(tab[1], idx[:, d * V:(d + 1) * V]) + f64(t) for d in range(D)]
    e = [np.exp(np.maximum(v, 0.2 * v)) for v in a]
    x = sum(e[d] * look(tab[0], idx[:, d * V:(d + 1) * V]) for d in range(D)) / sum(e)
    return x

@@ -1,0 +1,79 @@
+import concourse.mybir as mybir
+
+P = 128
+BLOCKS = 2
+NODES = 2048
+TARGETS = 1024
+CHUNK = 512
+CHUNKS = TARGETS // CHUNK
+SLOPE = 0.2
+
+F32, U16 = mybir.dt.float32, mybir.dt.uint16
+ADD, SUB, MUL, MAX = (
+    mybir.AluOpType.add,
+    mybir.AluOpType.subtract,
+    mybir.AluOpType.mult,
+    mybir.AluOpType.max,
+)
+SIGMOID = mybir.ActivationFunctionType.Sigmoid
+
+BYTES = 4 * (2 * 256 * NODES + 2 * 256 * TARGETS) + 2 * P * P
+
+
+def tile_lookup_gat_out_kernel(tc, tab, t, offs, out):
+    nc = tc.nc
+    with tc.tile_pool(name="held", bufs=1) as held, tc.tile_pool(name="ring", bufs=4) as ring:
+        offsets = held.tile([P, BLOCKS * TARGETS // 16], U16, name="offsets")
+        nc.sync.dma_start(offsets[:], offs)
+
+        def entries(d, c):
+            first = (d * TARGETS + c * CHUNK) // 16
+            return offsets[:, first : first + CHUNK // 16]
+
+        def columns(c):
+            return slice(c * CHUNK, (c + 1) * CHUNK)
+
+        def rows(b):
+            return slice(b * P, (b + 1) * P)
+
+        scores = [held.tile([P, NODES], F32, name=f"scores{b}") for b in range(BLOCKS)]
+        values = [held.tile([P, NODES], F32, name=f"values{b}") for b in range(BLOCKS)]
+        targets = [held.tile([P, TARGETS], F32, name=f"targets{b}") for b in range(BLOCKS)]
+        for b in range(BLOCKS):
+            nc.sync.dma_start(targets[b][:, columns(0)], t[rows(b), columns(0)])
+            nc.sync.dma_start(scores[b][:], tab[1, rows(b), :])
+            nc.sync.dma_start(targets[b][:, columns(1)], t[rows(b), columns(1)])
+        for b in range(BLOCKS):
+            nc.sync.dma_start(values[b][:], tab[0, rows(b), :])
+
+        weights = {}
+        for b in range(BLOCKS):
+            for c in range(CHUNKS):
+                leaky = []
+                for d in range(2):
+                    a = ring.tile([P, CHUNK], F32, name=f"a{d}")
+                    nc.vector.tensor_tensor(
+                        a[:], scores[b][:].indirect(entries(d, c)), targets[b][:, columns(c)], ADD
+                    )
+                    ramp = ring.tile([P, CHUNK], F32, name=f"ramp{d}")
+                    nc.vector.scalar_tensor_tensor(ramp[:], a[:], SLOPE, a[:], MUL, MAX)
+                    leaky.append(ramp)
+                lead = ring.tile([P, CHUNK], F32, name="lead")
+                nc.vector.tensor_tensor(lead[:], leaky[0][:], leaky[1][:], SUB)
+                for d, sign in ((0, 1.0), (1, -1.0)):
+                    w = held.tile([P, CHUNK], F32, name=f"weight{d}_{b}_{c}")
+                    nc.scalar.activation(w[:], lead[:], SIGMOID, scale=sign)
+                    weights[b, c, d] = w
+
+        for b in range(BLOCKS):
+            for c in range(CHUNKS):
+                parts = []
+                for d in range(2):
+                    part = ring.tile([P, CHUNK], F32, name=f"part{d}")
+                    nc.vector.tensor_tensor(
+                        part[:], values[b][:].indirect(entries(d, c)), weights[b, c, d][:], MUL
+                    )
+                    parts.append(part)
+                x = ring.tile([P, CHUNK], F32, name="x")
+                nc.vector.tensor_tensor(x[:], parts[0][:], parts[1][:], ADD)
+                nc.sync.dma_start(out[rows(b), columns(c)], x[:])

@@ -1,7 +1,9 @@
+import concourse.masks as masks
 import concourse.mybir as mybir
 
 P = 128
 BLOCKS = 2
+NEIGHBOURS = 2
 NODES = 2048
 TARGETS = 1024
 CHUNK = 512
@@ -9,21 +11,20 @@ CHUNKS = TARGETS // CHUNK
 SLOPE = 0.2
 
 F32, U16 = mybir.dt.float32, mybir.dt.uint16
-ADD, SUB, MUL, MAX = (
-    mybir.AluOpType.add,
-    mybir.AluOpType.subtract,
-    mybir.AluOpType.mult,
-    mybir.AluOpType.max,
-)
-SIGMOID = mybir.ActivationFunctionType.Sigmoid
+ADD, MUL = mybir.AluOpType.add, mybir.AluOpType.mult
+RELU, SIGMOID = mybir.ActivationFunctionType.Relu, mybir.ActivationFunctionType.Sigmoid
+
+FLOPS = 14 * 256 * TARGETS
 
 BYTES = 4 * (2 * 256 * NODES + 2 * 256 * TARGETS) + 2 * P * P
 
 
 def tile_lookup_gat_out_kernel(tc, tab, t, offs, out):
     nc = tc.nc
-    with tc.tile_pool(name="held", bufs=1) as held, tc.tile_pool(name="ring", bufs=4) as ring:
-        offsets = held.tile([P, BLOCKS * TARGETS // 16], U16, name="offsets")
+    with tc.tile_pool(name="held", bufs=1) as held, tc.tile_pool(name="ring", bufs=4) as ring, tc.psum_pool(
+        name="sums", bufs=4
+    ) as sums:
+        offsets = held.tile([P, NEIGHBOURS * TARGETS // 16], U16, name="offsets")
         nc.sync.dma_start(offsets[:], offs)
 
         def entries(d, c):
@@ -46,21 +47,27 @@ def tile_lookup_gat_out_kernel(tc, tab, t, offs, out):
         for b in range(BLOCKS):
             nc.sync.dma_start(values[b][:], tab[0, rows(b), :])
 
+        identity = held.tile([P, P], F32, name="identity")
+        masks.make_identity(nc, identity[:])
+        negative = held.tile([P, P], F32, name="negative")
+        nc.vector.tensor_scalar_mul(negative[:], identity[:], -1.0)
+        signed_identity = (identity, negative)
+
         weights = {}
         for b in range(BLOCKS):
             for c in range(CHUNKS):
-                leaky = []
-                for d in range(2):
+                lead = sums.tile([P, CHUNK], F32, name="lead")
+                for d in range(NEIGHBOURS):
                     a = ring.tile([P, CHUNK], F32, name=f"a{d}")
                     nc.vector.tensor_tensor(
                         a[:], scores[b][:].indirect(entries(d, c)), targets[b][:, columns(c)], ADD
                     )
                     ramp = ring.tile([P, CHUNK], F32, name=f"ramp{d}")
-                    nc.vector.scalar_tensor_tensor(ramp[:], a[:], SLOPE, a[:], MUL, MAX)
-                    leaky.append(ramp)
-                lead = ring.tile([P, CHUNK], F32, name="lead")
-                nc.vector.tensor_tensor(lead[:], leaky[0][:], leaky[1][:], SUB)
-                for d, sign in ((0, 1.0), (1, -1.0)):
+                    nc.scalar.activation(ramp[:], a[:], RELU, scale=(1.0 - SLOPE) / SLOPE)
+                    last = d == NEIGHBOURS - 1
+                    nc.tensor.matmul(lead[:], signed_identity[d][:], a[:], start=d == 0, stop=False)
+                    nc.tensor.matmul(lead[:], signed_identity[d][:], ramp[:], start=False, stop=last)
+                for d, sign in ((0, SLOPE), (1, -SLOPE)):
                     w = held.tile([P, CHUNK], F32, name=f"weight{d}_{b}_{c}")
                     nc.scalar.activation(w[:], lead[:], SIGMOID, scale=sign)
                     weights[b, c, d] = w
@@ -68,7 +75,7 @@ def tile_lookup_gat_out_kernel(tc, tab, t, offs, out):
         for b in range(BLOCKS):
             for c in range(CHUNKS):
                 parts = []
-                for d in range(2):
+                for d in range(NEIGHBOURS):
                     part = ring.tile([P, CHUNK], F32, name=f"part{d}")
                     nc.vector.tensor_tensor(
                         part[:], values[b][:].indirect(entries(d, c)), weights[b, c, d][:], MUL

@@ -11,7 +11,7 @@ CHUNKS = TARGETS // CHUNK
 SLOPE = 0.2
 
 F32, U16 = mybir.dt.float32, mybir.dt.uint16
-ADD, MUL = mybir.AluOpType.add, mybir.AluOpType.mult
+ADD, MUL, MAX = mybir.AluOpType.add, mybir.AluOpType.mult, mybir.AluOpType.max
 RELU, SIGMOID = mybir.ActivationFunctionType.Relu, mybir.ActivationFunctionType.Sigmoid
 
 FLOPS = 14 * 256 * TARGETS
@@ -62,11 +62,16 @@ def tile_lookup_gat_out_kernel(tc, tab, t, offs, out):
                     nc.vector.tensor_tensor(
                         a[:], scores[b][:].indirect(entries(d, c)), targets[b][:, columns(c)], ADD
                     )
-                    ramp = ring.tile([P, CHUNK], F32, name=f"ramp{d}")
-                    nc.scalar.activation(ramp[:], a[:], RELU, scale=(1.0 - SLOPE) / SLOPE)
-                    last = d == NEIGHBOURS - 1
-                    nc.tensor.matmul(lead[:], signed_identity[d][:], a[:], start=d == 0, stop=False)
-                    nc.tensor.matmul(lead[:], signed_identity[d][:], ramp[:], start=False, stop=last)
+                    sign_d, first, last = signed_identity[d][:], d == 0, d == NEIGHBOURS - 1
+                    if b == BLOCKS - 1 and d == NEIGHBOURS - 1:
+                        leaky = ring.tile([P, CHUNK], F32, name="leaky")
+                        nc.vector.scalar_tensor_tensor(leaky[:], a[:], 1.0 / SLOPE, a[:], MUL, MAX)
+                        nc.tensor.matmul(lead[:], sign_d, leaky[:], start=first, stop=last)
+                    else:
+                        ramp = ring.tile([P, CHUNK], F32, name=f"ramp{d}")
+                        nc.scalar.activation(ramp[:], a[:], RELU, scale=(1.0 - SLOPE) / SLOPE)
+                        nc.tensor.matmul(lead[:], sign_d, a[:], start=first, stop=False)
+                        nc.tensor.matmul(lead[:], sign_d, ramp[:], start=False, stop=last)
                 for d, sign in ((0, SLOPE), (1, -SLOPE)):
                     w = held.tile([P, CHUNK], F32, name=f"weight{d}_{b}_{c}")
                     nc.scalar.activation(w[:], lead[:], SIGMOID, scale=sign)

@@ -63,8 +63,8 @@ def tile_lookup_gat_out_kernel(tc, tab, t, offs, out):
                         a[:], scores[b][:].indirect(entries(d, c)), targets[b][:, columns(c)], ADD
                     )
                     sign_d, first, last = signed_identity[d][:], d == 0, d == NEIGHBOURS - 1
-                    if b == BLOCKS - 1 and d == NEIGHBOURS - 1:
-                        leaky = ring.tile([P, CHUNK], F32, name="leaky")
+                    if (b, c) == (BLOCKS - 1, CHUNKS - 1):
+                        leaky = ring.tile([P, CHUNK], F32, name=f"leaky{d}")
                         nc.vector.scalar_tensor_tensor(leaky[:], a[:], 1.0 / SLOPE, a[:], MUL, MAX)
                         nc.tensor.matmul(lead[:], sign_d, leaky[:], start=first, stop=last)
                     else:
@@ -77,15 +77,25 @@ def tile_lookup_gat_out_kernel(tc, tab, t, offs, out):
                     nc.scalar.activation(w[:], lead[:], SIGMOID, scale=sign)
                     weights[b, c, d] = w
 
+        def weighted(b, c, d, pieces):
+            part = ring.tile([P, CHUNK], F32, name=f"part{d}")
+            width = CHUNK // pieces
+            for i in range(pieces):
+                piece = slice(i * width, (i + 1) * width)
+                first = (d * TARGETS + c * CHUNK + i * width) // 16
+                picked = values[b][:].indirect(offsets[:, first : first + width // 16])
+                nc.vector.tensor_tensor(part[:, piece], picked, weights[b, c, d][:, piece], MUL)
+            return part
+
         for b in range(BLOCKS):
             for c in range(CHUNKS):
-                parts = []
-                for d in range(NEIGHBOURS):
-                    part = ring.tile([P, CHUNK], F32, name=f"part{d}")
-                    nc.vector.tensor_tensor(
-                        part[:], values[b][:].indirect(entries(d, c)), weights[b, c, d][:], MUL
-                    )
-                    parts.append(part)
+                pieces = 2 if (b, c) == (BLOCKS - 1, CHUNKS - 1) else 1
+                part0 = weighted(b, c, 0, 1)
+                part1 = weighted(b, c, 1, pieces)
                 x = ring.tile([P, CHUNK], F32, name="x")
-                nc.vector.tensor_tensor(x[:], parts[0][:], parts[1][:], ADD)
-                nc.sync.dma_start(out[rows(b), columns(c)], x[:])
+                width = CHUNK // pieces
+                for i in range(pieces):
+                    piece = slice(i * width, (i + 1) * width)
+                    goal = slice(c * CHUNK + i * width, c * CHUNK + (i + 1) * width)
+                    nc.vector.tensor_tensor(x[:, piece], part0[:, piece], part1[:, piece], ADD)
+                    nc.sync.dma_start(out[rows(b), goal], x[:, piece])

import concourse.masks as masks
import concourse.mybir as mybir

P = 128
BLOCKS = 2
NEIGHBOURS = 2
NODES = 2048
TARGETS = 1024
CHUNK = 512
CHUNKS = TARGETS // CHUNK
SLOPE = 0.2

F32, U16 = mybir.dt.float32, mybir.dt.uint16
ADD, MUL, MAX = mybir.AluOpType.add, mybir.AluOpType.mult, mybir.AluOpType.max
RELU, SIGMOID = mybir.ActivationFunctionType.Relu, mybir.ActivationFunctionType.Sigmoid

FLOPS = 14 * 256 * TARGETS

BYTES = 4 * (2 * 256 * NODES + 2 * 256 * TARGETS) + 2 * P * P


def tile_lookup_gat_out_kernel(tc, tab, t, offs, out):
    nc = tc.nc
    with tc.tile_pool(name="held", bufs=1) as held, tc.tile_pool(name="ring", bufs=4) as ring, tc.psum_pool(
        name="sums", bufs=4
    ) as sums:
        offsets = held.tile([P, NEIGHBOURS * TARGETS // 16], U16, name="offsets")
        nc.sync.dma_start(offsets[:], offs)

        def entries(d, c):
            first = (d * TARGETS + c * CHUNK) // 16
            return offsets[:, first : first + CHUNK // 16]

        def columns(c):
            return slice(c * CHUNK, (c + 1) * CHUNK)

        def rows(b):
            return slice(b * P, (b + 1) * P)

        scores = [held.tile([P, NODES], F32, name=f"scores{b}") for b in range(BLOCKS)]
        values = [held.tile([P, NODES], F32, name=f"values{b}") for b in range(BLOCKS)]
        targets = [held.tile([P, TARGETS], F32, name=f"targets{b}") for b in range(BLOCKS)]
        for b in range(BLOCKS):
            nc.sync.dma_start(targets[b][:, columns(0)], t[rows(b), columns(0)])
            nc.sync.dma_start(scores[b][:], tab[1, rows(b), :])
            nc.sync.dma_start(targets[b][:, columns(1)], t[rows(b), columns(1)])
        for b in range(BLOCKS):
            nc.sync.dma_start(values[b][:], tab[0, rows(b), :])

        identity = held.tile([P, P], F32, name="identity")
        masks.make_identity(nc, identity[:])
        negative = held.tile([P, P], F32, name="negative")
        nc.vector.tensor_scalar_mul(negative[:], identity[:], -1.0)
        signed_identity = (identity, negative)

        weights = {}
        for b in range(BLOCKS):
            for c in range(CHUNKS):
                lead = sums.tile([P, CHUNK], F32, name="lead")
                for d in range(NEIGHBOURS):
                    a = ring.tile([P, CHUNK], F32, name=f"a{d}")
                    nc.vector.tensor_tensor(
                        a[:], scores[b][:].indirect(entries(d, c)), targets[b][:, columns(c)], ADD
                    )
                    sign_d, first, last = signed_identity[d][:], d == 0, d == NEIGHBOURS - 1
                    if (b, c) == (BLOCKS - 1, CHUNKS - 1):
                        leaky = ring.tile([P, CHUNK], F32, name=f"leaky{d}")
                        nc.vector.scalar_tensor_tensor(leaky[:], a[:], 1.0 / SLOPE, a[:], MUL, MAX)
                        nc.tensor.matmul(lead[:], sign_d, leaky[:], start=first, stop=last)
                    else:
                        ramp = ring.tile([P, CHUNK], F32, name=f"ramp{d}")
                        nc.scalar.activation(ramp[:], a[:], RELU, scale=(1.0 - SLOPE) / SLOPE)
                        nc.tensor.matmul(lead[:], sign_d, a[:], start=first, stop=False)
                        nc.tensor.matmul(lead[:], sign_d, ramp[:], start=False, stop=last)
                for d, sign in ((0, SLOPE), (1, -SLOPE)):
                    w = held.tile([P, CHUNK], F32, name=f"weight{d}_{b}_{c}")
                    nc.scalar.activation(w[:], lead[:], SIGMOID, scale=sign)
                    weights[b, c, d] = w

        def weighted(b, c, d, pieces):
            part = ring.tile([P, CHUNK], F32, name=f"part{d}")
            width = CHUNK // pieces
            for i in range(pieces):
                piece = slice(i * width, (i + 1) * width)
                first = (d * TARGETS + c * CHUNK + i * width) // 16
                picked = values[b][:].indirect(offsets[:, first : first + width // 16])
                nc.vector.tensor_tensor(part[:, piece], picked, weights[b, c, d][:, piece], MUL)
            return part

        for b in range(BLOCKS):
            for c in range(CHUNKS):
                pieces = 2 if (b, c) == (BLOCKS - 1, CHUNKS - 1) else 1
                part0 = weighted(b, c, 0, 1)
                part1 = weighted(b, c, 1, pieces)
                x = ring.tile([P, CHUNK], F32, name="x")
                width = CHUNK // pieces
                for i in range(pieces):
                    piece = slice(i * width, (i + 1) * width)
                    goal = slice(c * CHUNK + i * width, c * CHUNK + (i + 1) * width)
                    nc.vector.tensor_tensor(x[:, piece], part0[:, piece], part1[:, piece], ADD)
                    nc.sync.dma_start(out[rows(b), goal], x[:, piece])
